import numpy as np
import ml_dtypes


def mxq(x, axis, fmt="e4m3"):
    dtype, down = {"e4m3": (ml_dtypes.float8_e4m3fn, 7), "e5m2": (ml_dtypes.float8_e5m2, 14)}[fmt]
    v = np.moveaxis(np.asarray(x, np.float32).astype(ml_dtypes.bfloat16).astype(np.float64), axis, -1)
    blocks = v.reshape(v.shape[:-1] + (-1, 32))
    amax = np.abs(blocks).max(-1, keepdims=True)
    byte = np.maximum(np.where(amax > 0, np.frexp(amax)[1] - 1 + 127, 0) - down, 1)
    scale = np.exp2(byte - 127.0)
    codes = (blocks / scale).astype(np.float32).astype(dtype).astype(np.float64)
    return np.moveaxis((codes * scale).reshape(v.shape), -1, axis)


WIDE = False


def mx_kscale(k):
    if not WIDE:
        return np.ones(k)
    levels = np.array([10, -10, 5, -5, 0])
    if k % 512:
        return np.exp2(np.random.permutation(np.resize(levels, k // 32))).repeat(32)
    a = np.empty((k // 512, 16))
    for p in range(k // 512):
        a[p, :8] = np.random.permutation(np.resize(levels, 8))
        for g in range(8):
            far = levels[np.abs(levels - a[p, g]) >= 10]
            a[p, g + 8] = far[np.random.randint(len(far))]
    return np.exp2(a.ravel()).repeat(32)


def f64(x):
    return np.asarray(x).astype(np.float64)


def striped8(idx):
    return np.asarray(idx).reshape(8, -1, 16).transpose(0, 2, 1).reshape(128, -1).astype(np.uint16)


def unstriped8(offs):
    return offs.reshape(8, 16, -1).transpose(0, 2, 1).reshape(8, -1).astype(np.int64)


def pick8(x, idx, run):
    r = np.arange(len(x))
    return x[r[:, None], idx[r % (8 * run) // run]]


E2M1 = np.array([0.0, 0.5, 1.0, 1.5, 2.0, 3.0, 4.0, 6.0, -0.0, -0.5, -1.0, -1.5, -2.0, -3.0, -4.0, -6.0])


def pack_weight(w, fmt):
    k, n = w.shape
    w = f64(np.asarray(w, np.float32).astype(ml_dtypes.bfloat16)).reshape(k // 32, 32, n)
    amax = np.abs(w).max(1)
    if fmt == "e4m3":
        byte = np.frexp(amax)[1] - 1 + 127 - 7
    else:
        mant, ex = np.frexp(amax / 6.0)
        byte = np.where(mant > 0.5, ex, ex - 1) + 127
    byte = np.clip(np.where(amax > 0, byte, 1), 1, 254)
    scaled = (w * np.exp2(127.0 - byte)[:, None, :]).reshape(k, n).astype(np.float32)
    by_word = np.ascontiguousarray(scaled.reshape(k // 512, 128, 4, n).transpose(0, 1, 3, 2))
    if fmt == "e4m3":
        words = by_word.astype(ml_dtypes.float8_e4m3fn).view(np.uint8)
    else:
        c = by_word.astype(ml_dtypes.float4_e2m1fn).view(np.uint8) & 0xF
        words = (c[..., 0::2] | (c[..., 1::2] << 4)).reshape(k // 512, 128, 2 * n)
    return np.ascontiguousarray(words), np.ascontiguousarray(byte.astype(np.uint8).reshape(k // 512, 16, n))


def unpack_weight(words, scales, fmt):
    g, _, n = scales.shape
    words = np.ascontiguousarray(words).reshape(g, 128, n, -1)
    if fmt == "e4m3":
        vals = words.view(ml_dtypes.float8_e4m3fn).astype(np.float64)
    else:
        nib = np.empty((g, 128, n, 4), np.uint8)
        nib[..., 0::2] = words & 0xF
        nib[..., 1::2] = words >> 4
        vals = E2M1[nib]
    vals = vals * np.repeat(np.exp2(scales.astype(np.float64) - 127.0), 8, axis=1)[..., None]
    return vals.transpose(0, 1, 3, 2).reshape(g * 512, n)


D, T, I, Q = 512, 1024, 512, 128


def setup_inputs():
    n = np.random.standard_normal
    idx = np.stack([np.random.permutation(T)[:I] for _ in range(8)])
    idx2 = np.stack([np.random.permutation(T)[:I] for _ in range(8)])
    fd = mx_kscale(D)
    keysp = pack_weight(n((D, T)) / fd[:, None], "e2m1")
    return {
        "query": (n((D, Q)) * 0.9 / np.sqrt(D) * fd[:, None]).astype(np.float32),
        "query2": (n((D, Q)) * 0.9 / np.sqrt(D) * fd[:, None]).astype(np.float32),
        "keys_words": keysp[0],
        "keys_scales": keysp[1],
        "lam": (np.random.uniform(0.5, 1.5, (Q, 1))).astype(np.float32),
        "earlier": (np.random.uniform(0.1, 2.0, (Q, I))).astype(np.float32),
        "trust": (np.random.uniform(0.3, 0.8, (Q, 1))).astype(np.float32),
        "base": (0.3 * n((Q, I))).astype(np.float32),
        "gain2": (np.random.uniform(0.5, 2.0, (Q, 1))).astype(np.float32),
        "offs": striped8(idx),
        "offs2": striped8(idx2),
    }


def reference(query, query2, keys_words, keys_scales, lam, earlier, trust, base, gain2, offs, offs2):
    idx = unstriped8(offs)
    idx2 = unstriped8(offs2)
    keysu = unpack_weight(keys_words, keys_scales, "e2m1")
    queryq = mxq(f64(query), 0, "e4m3")
    a = queryq.T @ keysu
    query2q = mxq(f64(query2), 0, "e4m3")
    b = query2q.T @ keysu
    s = pick8(a, idx, 16) + pick8(a, idx2, 16) * np.tanh(pick8(b, idx, 16)) * f64(lam)
    p = np.exp(s - np.max(s, axis=1, keepdims=True))
    r = p / np.sum(p, axis=1, keepdims=True)
    re0 = f64(earlier) / np.sum(f64(earlier), axis=1, keepdims=True)
    w = r * f64(trust) + re0 * (1.0 - f64(trust))
    y = np.tanh(w * f64(gain2) * 256.0) + f64(base)
    return y

@@ -1,0 +1,166 @@
+from contextlib import ExitStack
+
+import concourse.mybir as mybir
+
+F32 = mybir.dt.float32
+BF16 = mybir.dt.bfloat16
+I32 = mybir.dt.int32
+U32 = mybir.dt.uint32
+U16 = mybir.dt.uint16
+U8 = mybir.dt.uint8
+FP8X4 = mybir.dt.float8_e4m3fn_x4
+FP4X4 = mybir.dt.float4_e2m1fn_x4
+ALU = mybir.AluOpType
+ACT = mybir.ActivationFunctionType
+AXIS = mybir.AxisListType
+
+P = 128
+PACK = 4
+D, T, SLOTS, Q = 512, 1024, 512, 128
+N_TILE = 256
+HALF = SLOTS // 2
+LIST_COLS = SLOTS // 16
+
+FLOPS = 2 * 2 * D * T * Q
+
+
+def quantize_query(nc, pool, raw, name):
+    grouped = pool.tile([P, Q, PACK], BF16, name=name + "_grouped", tag=name + "_grouped", align_bytes=64)
+    nc.vector.tensor_copy(out=grouped[:], in_=raw[:].rearrange("p j w -> p w j"))
+    codes = pool.tile([P, Q], U32, name=name + "_codes", tag=name + "_codes", align_bytes=64)
+    scales = pool.tile([P, Q], U8, name=name + "_scales", tag=name + "_scales", align_bytes=64)
+    nc.vector.quantize_mx(out=codes[:].bitcast(FP8X4), scales=scales[:], in_=grouped[:].rearrange("p w j -> p (w j)"))
+    return codes, scales
+
+
+def score_tokens(nc, psum, codes, scales, key_words, key_scales, scores, on_scalar, name):
+    banks = []
+    for c in range(T // N_TILE):
+        cols = slice(c * N_TILE, (c + 1) * N_TILE)
+        bank = psum.tile([P, N_TILE], F32, name="%s_bank%d" % (name, c), tag="%s_bank%d" % (name, c))
+        nc.tensor.matmul_mx(
+            out=bank[:],
+            lhsT=codes[:].bitcast(FP8X4),
+            lhsT_scale=scales[:],
+            rhs=key_words[c // 2][:, 2 * (c % 2) * N_TILE : 2 * (c % 2 + 1) * N_TILE].bitcast(FP4X4),
+            rhs_scale=key_scales[:, cols],
+            start=True,
+            stop=True,
+        )
+        if c < on_scalar:
+            nc.scalar.activation(out=scores[:, cols], in_=bank[:], func=ACT.Copy)
+        banks.append(bank)
+    return banks
+
+
+def tile_attend_turnedby_carried_gated_heads_kernel(
+    tc, query, query2, keys_words, keys_scales, lam, earlier, trust, base, gain2, offs, offs2, out
+):
+    nc = tc.nc
+    with ExitStack() as ctx:
+        pool = ctx.enter_context(tc.tile_pool(name="pool", bufs=1))
+        psum = ctx.enter_context(tc.psum_pool(name="psum", bufs=1))
+
+        key_scales = pool.tile([P, T], U8, name="key_scales", align_bytes=64)
+        nc.vector.memset(key_scales[:].bitcast(I32), 0)
+
+        q2_raw = pool.tile([P, PACK, Q], F32, name="q2_raw")
+        nc.sync.dma_start(out=q2_raw[:], in_=query2.rearrange("(p j) w -> p j w", j=PACK))
+        for quad in range(4):
+            (nc.sync if quad < 2 else nc.scalar).dma_start(
+                out=key_scales[32 * quad : 32 * quad + 4, :].bitcast(I32),
+                in_=keys_scales[0, 4 * quad : 4 * quad + 4, :].bitcast(I32),
+            )
+        words_lo = pool.tile([P, T], U8, name="words_lo", tag="words_lo", align_bytes=64)
+        nc.sync.dma_start(out=words_lo[:].bitcast(I32), in_=keys_words[0, :, 0:T].bitcast(I32))
+        q_raw = pool.tile([P, PACK, Q], F32, name="q_raw")
+        nc.sync.dma_start(out=q_raw[:], in_=query.rearrange("(p j) w -> p j w", j=PACK))
+        words_hi = pool.tile([P, T], U8, name="words_hi", tag="gate", align_bytes=64)
+        nc.sync.dma_start(out=words_hi[:].bitcast(I32), in_=keys_words[0, :, T : 2 * T].bitcast(I32))
+        key_words = [words_lo, words_hi]
+        list1 = pool.tile([P, LIST_COLS], U16, name="list1")
+        nc.sync.dma_start(list1[:], offs)
+        list2 = pool.tile([P, LIST_COLS], U16, name="list2")
+        nc.sync.dma_start(list2[:], offs2)
+
+        b = pool.tile([P, T], F32, name="b", tag="b")
+        a = pool.tile([P, T], F32, name="a")
+        q2_codes, q2_scales = quantize_query(nc, pool, q2_raw, "q2")
+        b_banks = score_tokens(nc, psum, q2_codes, q2_scales, key_words, key_scales, b, 3, "b")
+        q_codes, q_scales = quantize_query(nc, pool, q_raw, "q")
+        nc.vector.tensor_copy(out=b[:, 3 * N_TILE :], in_=b_banks[3][:])
+        score_tokens(nc, psum, q_codes, q_scales, key_words, key_scales, a, 4, "a")
+
+        lam_col = pool.tile([P, 1], F32, name="lam_col", tag="q2_codes", align_bytes=64)
+        nc.sync.dma_start(out=lam_col[:], in_=lam)
+        earlier_sb = pool.tile([P, SLOTS], F32, name="earlier_sb", tag="q2_scales", align_bytes=64)
+        nc.sync.dma_start(out=earlier_sb[:], in_=earlier)
+        trust_col = pool.tile([P, 1], F32, name="trust_col", tag="words_lo", align_bytes=64)
+        nc.sync.dma_start(out=trust_col[:], in_=trust)
+        gain_col = pool.tile([P, 1], F32, name="gain_col", tag="q_scales", align_bytes=64)
+        nc.sync.dma_start(out=gain_col[:], in_=gain2)
+
+        halves = [(slice(h * HALF, (h + 1) * HALF), slice(h * LIST_COLS // 2, (h + 1) * LIST_COLS // 2)) for h in range(2)]
+        gate = pool.tile([P, SLOTS], F32, name="gate", tag="gate", align_bytes=64)
+        b_picked = pool.tile([P, SLOTS], F32, name="b_picked", tag="q_grouped", align_bytes=64)
+        for h, (cols, entries) in enumerate(halves):
+            nc.vector.tensor_copy(out=b_picked[:, cols], in_=b[:].indirect(list1[:, entries]))
+            nc.scalar.activation(out=gate[:, cols], in_=b_picked[:, cols], func=ACT.Tanh)
+        base_sb = pool.tile([P, SLOTS], F32, name="base_sb", tag="b")
+        nc.sync.dma_start(out=base_sb[:], in_=base)
+        turned = pool.tile([P, SLOTS], F32, name="turned")
+        a_picked = pool.tile([P, SLOTS], F32, name="a_picked")
+        for h, (cols, entries) in enumerate(halves):
+            nc.vector.tensor_tensor(out=turned[:, cols], in0=a[:].indirect(list2[:, entries]), in1=gate[:, cols], op=ALU.mult)
+            nc.scalar.activation(out=a_picked[:, cols], in_=a[:].indirect(list1[:, entries]), func=ACT.Copy)
+
+        score = pool.tile([P, SLOTS], F32, name="score")
+        neg_score = pool.tile([P, SLOTS], F32, name="neg_score")
+        neg_max = [pool.tile([P, 1], F32, name="neg_max%d" % h) for h in range(2)]
+        for h, (cols, entries) in enumerate(halves):
+            nc.vector.scalar_tensor_tensor(
+                out=score[:, cols], in0=turned[:, cols], scalar=lam_col[:], in1=a_picked[:, cols], op0=ALU.mult, op1=ALU.add
+            )
+            nc.vector.tensor_scalar(
+                out=neg_score[:, cols],
+                in0=score[:, cols],
+                scalar1=-1.0,
+                scalar2=neg_max[h - 1][:] if h else None,
+                op0=ALU.mult,
+                op1=ALU.min,
+                accum_out=neg_max[h][:],
+            )
+
+        old_sum = pool.tile([P, 1], F32, name="old_sum")
+        old = pool.tile([P, SLOTS], F32, name="old", tag="gate", align_bytes=64)
+        nc.scalar.activation(out=old[:], in_=earlier_sb[:], func=ACT.Copy, accum_out=old_sum[:])
+        old_inv = pool.tile([P, 1], F32, name="old_inv")
+        nc.vector.reciprocal(out=old_inv[:], in_=old_sum[:])
+        old_share = pool.tile([P, 1], F32, name="old_share")
+        nc.vector.scalar_tensor_tensor(
+            out=old_share[:], in0=trust_col[:], scalar=-1.0, in1=old_inv[:], op0=ALU.add, op1=ALU.mult
+        )
+        carried = pool.tile([P, SLOTS], F32, name="carried")
+        nc.vector.tensor_scalar(
+            out=carried[:], in0=old[:], scalar1=old_share[:], scalar2=-256.0, op0=ALU.mult, op1=ALU.mult
+        )
+
+        p = pool.tile([P, SLOTS], F32, name="p")
+        p_sum = pool.tile([P, 1], F32, name="p_sum")
+        nc.scalar.activation(out=p[:], in_=neg_score[:], func=ACT.Exp, scale=-1.0, bias=neg_max[1][:], accum_out=p_sum[:])
+        p_inv = pool.tile([P, 1], F32, name="p_inv")
+        nc.vector.reciprocal(out=p_inv[:], in_=p_sum[:])
+        p_gain = pool.tile([P, 1], F32, name="p_gain")
+        nc.vector.tensor_scalar(out=p_gain[:], in0=p_inv[:], scalar1=trust_col[:], scalar2=256.0, op0=ALU.mult, op1=ALU.mult)
+
+        blend = pool.tile([P, SLOTS], F32, name="blend")
+        squashed = pool.tile([P, SLOTS], F32, name="squashed")
+        result = pool.tile([P, SLOTS], F32, name="result")
+        for cols in (slice(0, 192), slice(192, 384), slice(384, 512)):
+            nc.vector.scalar_tensor_tensor(
+                out=blend[:, cols], in0=p[:, cols], scalar=p_gain[:], in1=carried[:, cols], op0=ALU.mult, op1=ALU.add
+            )
+            nc.scalar.activation(out=squashed[:, cols], in_=blend[:, cols], func=ACT.Tanh, scale=gain_col[:])
+        for cols in (slice(0, 192), slice(192, 384), slice(384, 512)):
+            nc.vector.tensor_tensor(out=result[:, cols], in0=squashed[:, cols], in1=base_sb[:, cols], op=ALU.add)
+            nc.sync.dma_start(out=out[:, cols], in_=result[:, cols])

@@ -26,10 +26,15 @@ FLOPS = 2 * 2 * D * T * Q
 
 def quantize_query(nc, pool, raw, name):
     grouped = pool.tile([P, Q, PACK], BF16, name=name + "_grouped", tag=name + "_grouped", align_bytes=64)
-    nc.vector.tensor_copy(out=grouped[:], in_=raw[:].rearrange("p j w -> p w j"))
     codes = pool.tile([P, Q], U32, name=name + "_codes", tag=name + "_codes", align_bytes=64)
     scales = pool.tile([P, Q], U8, name=name + "_scales", tag=name + "_scales", align_bytes=64)
-    nc.vector.quantize_mx(out=codes[:].bitcast(FP8X4), scales=scales[:], in_=grouped[:].rearrange("p w j -> p (w j)"))
+    parts = [slice(0, Q // 2), slice(Q // 2, Q)]
+    for rows in parts:
+        nc.vector.tensor_copy(out=grouped[:, rows, :], in_=raw[:, :, rows].rearrange("p j w -> p w j"))
+    for rows in parts:
+        nc.vector.quantize_mx(
+            out=codes[:, rows].bitcast(FP8X4), scales=scales[:, rows], in_=grouped[:, rows, :].rearrange("p w j -> p (w j)")
+        )
     return codes, scales
 
 
@@ -102,34 +107,31 @@ def tile_attend_turnedby_carried_gated_heads_kernel(
 
         halves = [(slice(h * HALF, (h + 1) * HALF), slice(h * LIST_COLS // 2, (h + 1) * LIST_COLS // 2)) for h in range(2)]
         gate = pool.tile([P, SLOTS], F32, name="gate", tag="gate", align_bytes=64)
-        b_picked = pool.tile([P, SLOTS], F32, name="b_picked", tag="q_grouped", align_bytes=64)
+        b_picked = [
+            pool.tile([P, HALF], F32, name="b_picked0", tag="q_grouped", align_bytes=64),
+            pool.tile([P, HALF], F32, name="b_picked1"),
+        ]
         for h, (cols, entries) in enumerate(halves):
-            nc.vector.tensor_copy(out=b_picked[:, cols], in_=b[:].indirect(list1[:, entries]))
-            nc.scalar.activation(out=gate[:, cols], in_=b_picked[:, cols], func=ACT.Tanh)
+            nc.vector.tensor_copy(out=b_picked[h][:], in_=b[:].indirect(list1[:, entries]))
+        for h, (cols, entries) in enumerate(halves):
+            nc.scalar.activation(out=gate[:, cols], in_=b_picked[h][:], func=ACT.Tanh)
         base_sb = pool.tile([P, SLOTS], F32, name="base_sb", tag="b")
         nc.sync.dma_start(out=base_sb[:], in_=base)
-        turned = pool.tile([P, SLOTS], F32, name="turned")
+        turned = pool.tile([P, SLOTS], F32, name="turned", tag="turned")
         a_picked = pool.tile([P, SLOTS], F32, name="a_picked")
         for h, (cols, entries) in enumerate(halves):
             nc.vector.tensor_tensor(out=turned[:, cols], in0=a[:].indirect(list2[:, entries]), in1=gate[:, cols], op=ALU.mult)
             nc.scalar.activation(out=a_picked[:, cols], in_=a[:].indirect(list1[:, entries]), func=ACT.Copy)
 
         score = pool.tile([P, SLOTS], F32, name="score")
-        neg_score = pool.tile([P, SLOTS], F32, name="neg_score")
-        neg_max = [pool.tile([P, 1], F32, name="neg_max%d" % h) for h in range(2)]
         for h, (cols, entries) in enumerate(halves):
             nc.vector.scalar_tensor_tensor(
                 out=score[:, cols], in0=turned[:, cols], scalar=lam_col[:], in1=a_picked[:, cols], op0=ALU.mult, op1=ALU.add
             )
-            nc.vector.tensor_scalar(
-                out=neg_score[:, cols],
-                in0=score[:, cols],
-                scalar1=-1.0,
-                scalar2=neg_max[h - 1][:] if h else None,
-                op0=ALU.mult,
-                op1=ALU.min,
-                accum_out=neg_max[h][:],
-            )
+        new_share = pool.tile([P, 1], F32, name="new_share", tag="turned")
+        nc.vector.tensor_scalar(out=new_share[:], in0=trust_col[:], scalar1=256.0, scalar2=None, op0=ALU.mult)
+        neg_max = pool.tile([P, 1], F32, name="neg_max")
+        nc.vector.tensor_reduce(out=neg_max[:], in_=score[:], axis=AXIS.X, op=ALU.max, negate=True)
 
         old_sum = pool.tile([P, 1], F32, name="old_sum")
         old = pool.tile([P, SLOTS], F32, name="old", tag="gate", align_bytes=64)
@@ -147,20 +149,24 @@ def tile_attend_turnedby_carried_gated_heads_kernel(
 
         p = pool.tile([P, SLOTS], F32, name="p")
         p_sum = pool.tile([P, 1], F32, name="p_sum")
-        nc.scalar.activation(out=p[:], in_=neg_score[:], func=ACT.Exp, scale=-1.0, bias=neg_max[1][:], accum_out=p_sum[:])
+        nc.scalar.activation(out=p[:], in_=score[:], func=ACT.Exp, bias=neg_max[:], accum_out=p_sum[:])
         p_inv = pool.tile([P, 1], F32, name="p_inv")
         nc.vector.reciprocal(out=p_inv[:], in_=p_sum[:])
-        p_gain = pool.tile([P, 1], F32, name="p_gain")
-        nc.vector.tensor_scalar(out=p_gain[:], in0=p_inv[:], scalar1=trust_col[:], scalar2=256.0, op0=ALU.mult, op1=ALU.mult)
 
+        trusted = pool.tile([P, SLOTS], F32, name="trusted")
         blend = pool.tile([P, SLOTS], F32, name="blend")
         squashed = pool.tile([P, SLOTS], F32, name="squashed")
         result = pool.tile([P, SLOTS], F32, name="result")
-        for cols in (slice(0, 192), slice(192, 384), slice(384, 512)):
+        pieces = [slice(c, c + 128) for c in range(0, SLOTS, 128)]
+        for cols in pieces:
+            nc.scalar.activation(out=trusted[:, cols], in_=p[:, cols], func=ACT.Copy, scale=new_share[:])
+        for cols in pieces:
             nc.vector.scalar_tensor_tensor(
-                out=blend[:, cols], in0=p[:, cols], scalar=p_gain[:], in1=carried[:, cols], op0=ALU.mult, op1=ALU.add
+                out=blend[:, cols], in0=trusted[:, cols], scalar=p_inv[:], in1=carried[:, cols], op0=ALU.mult, op1=ALU.add
             )
             nc.scalar.activation(out=squashed[:, cols], in_=blend[:, cols], func=ACT.Tanh, scale=gain_col[:])
-        for cols in (slice(0, 192), slice(192, 384), slice(384, 512)):
+        for n, cols in enumerate(pieces):
             nc.vector.tensor_tensor(out=result[:, cols], in0=squashed[:, cols], in1=base_sb[:, cols], op=ALU.add)
-            nc.sync.dma_start(out=out[:, cols], in_=result[:, cols])
+            if n > 0:
+                stored = slice(0, 256) if n == 1 else cols
+                nc.sync.dma_start(out=out[:, stored], in_=result[:, stored])

from contextlib import ExitStack

import concourse.mybir as mybir

F32 = mybir.dt.float32
BF16 = mybir.dt.bfloat16
I32 = mybir.dt.int32
U32 = mybir.dt.uint32
U16 = mybir.dt.uint16
U8 = mybir.dt.uint8
FP8X4 = mybir.dt.float8_e4m3fn_x4
FP4X4 = mybir.dt.float4_e2m1fn_x4
ALU = mybir.AluOpType
ACT = mybir.ActivationFunctionType
AXIS = mybir.AxisListType

P = 128
PACK = 4
D, T, SLOTS, Q = 512, 1024, 512, 128
N_TILE = 256
HALF = SLOTS // 2
LIST_COLS = SLOTS // 16

FLOPS = 2 * 2 * D * T * Q


def quantize_query(nc, pool, raw, name):
    grouped = pool.tile([P, Q, PACK], BF16, name=name + "_grouped", tag=name + "_grouped", align_bytes=64)
    codes = pool.tile([P, Q], U32, name=name + "_codes", tag=name + "_codes", align_bytes=64)
    scales = pool.tile([P, Q], U8, name=name + "_scales", tag=name + "_scales", align_bytes=64)
    parts = [slice(0, Q // 2), slice(Q // 2, Q)]
    for rows in parts:
        nc.vector.tensor_copy(out=grouped[:, rows, :], in_=raw[:, :, rows].rearrange("p j w -> p w j"))
    for rows in parts:
        nc.vector.quantize_mx(
            out=codes[:, rows].bitcast(FP8X4), scales=scales[:, rows], in_=grouped[:, rows, :].rearrange("p w j -> p (w j)")
        )
    return codes, scales


def score_tokens(nc, psum, codes, scales, key_words, key_scales, scores, on_scalar, name):
    banks = []
    for c in range(T // N_TILE):
        cols = slice(c * N_TILE, (c + 1) * N_TILE)
        bank = psum.tile([P, N_TILE], F32, name="%s_bank%d" % (name, c), tag="%s_bank%d" % (name, c))
        nc.tensor.matmul_mx(
            out=bank[:],
            lhsT=codes[:].bitcast(FP8X4),
            lhsT_scale=scales[:],
            rhs=key_words[c // 2][:, 2 * (c % 2) * N_TILE : 2 * (c % 2 + 1) * N_TILE].bitcast(FP4X4),
            rhs_scale=key_scales[:, cols],
            start=True,
            stop=True,
        )
        if c < on_scalar:
            nc.scalar.activation(out=scores[:, cols], in_=bank[:], func=ACT.Copy)
        banks.append(bank)
    return banks


def tile_attend_turnedby_carried_gated_heads_kernel(
    tc, query, query2, keys_words, keys_scales, lam, earlier, trust, base, gain2, offs, offs2, out
):
    nc = tc.nc
    with ExitStack() as ctx:
        pool = ctx.enter_context(tc.tile_pool(name="pool", bufs=1))
        psum = ctx.enter_context(tc.psum_pool(name="psum", bufs=1))

        key_scales = pool.tile([P, T], U8, name="key_scales", align_bytes=64)
        nc.vector.memset(key_scales[:].bitcast(I32), 0)

        q2_raw = pool.tile([P, PACK, Q], F32, name="q2_raw")
        nc.sync.dma_start(out=q2_raw[:], in_=query2.rearrange("(p j) w -> p j w", j=PACK))
        for quad in range(4):
            (nc.sync if quad < 2 else nc.scalar).dma_start(
                out=key_scales[32 * quad : 32 * quad + 4, :].bitcast(I32),
                in_=keys_scales[0, 4 * quad : 4 * quad + 4, :].bitcast(I32),
            )
        words_lo = pool.tile([P, T], U8, name="words_lo", tag="words_lo", align_bytes=64)
        nc.sync.dma_start(out=words_lo[:].bitcast(I32), in_=keys_words[0, :, 0:T].bitcast(I32))
        q_raw = pool.tile([P, PACK, Q], F32, name="q_raw")
        nc.sync.dma_start(out=q_raw[:], in_=query.rearrange("(p j) w -> p j w", j=PACK))
        words_hi = pool.tile([P, T], U8, name="words_hi", tag="gate", align_bytes=64)
        nc.sync.dma_start(out=words_hi[:].bitcast(I32), in_=keys_words[0, :, T : 2 * T].bitcast(I32))
        key_words = [words_lo, words_hi]
        list1 = pool.tile([P, LIST_COLS], U16, name="list1")
        nc.sync.dma_start(list1[:], offs)
        list2 = pool.tile([P, LIST_COLS], U16, name="list2")
        nc.sync.dma_start(list2[:], offs2)

        b = pool.tile([P, T], F32, name="b", tag="b")
        a = pool.tile([P, T], F32, name="a")
        q2_codes, q2_scales = quantize_query(nc, pool, q2_raw, "q2")
        b_banks = score_tokens(nc, psum, q2_codes, q2_scales, key_words, key_scales, b, 3, "b")
        q_codes, q_scales = quantize_query(nc, pool, q_raw, "q")
        nc.vector.tensor_copy(out=b[:, 3 * N_TILE :], in_=b_banks[3][:])
        score_tokens(nc, psum, q_codes, q_scales, key_words, key_scales, a, 4, "a")

        lam_col = pool.tile([P, 1], F32, name="lam_col", tag="q2_codes", align_bytes=64)
        nc.sync.dma_start(out=lam_col[:], in_=lam)
        earlier_sb = pool.tile([P, SLOTS], F32, name="earlier_sb", tag="q2_scales", align_bytes=64)
        nc.sync.dma_start(out=earlier_sb[:], in_=earlier)
        trust_col = pool.tile([P, 1], F32, name="trust_col", tag="words_lo", align_bytes=64)
        nc.sync.dma_start(out=trust_col[:], in_=trust)
        gain_col = pool.tile([P, 1], F32, name="gain_col", tag="q_scales", align_bytes=64)
        nc.sync.dma_start(out=gain_col[:], in_=gain2)

        halves = [(slice(h * HALF, (h + 1) * HALF), slice(h * LIST_COLS // 2, (h + 1) * LIST_COLS // 2)) for h in range(2)]
        gate = pool.tile([P, SLOTS], F32, name="gate", tag="gate", align_bytes=64)
        b_picked = [
            pool.tile([P, HALF], F32, name="b_picked0", tag="q_grouped", align_bytes=64),
            pool.tile([P, HALF], F32, name="b_picked1"),
        ]
        for h, (cols, entries) in enumerate(halves):
            nc.vector.tensor_copy(out=b_picked[h][:], in_=b[:].indirect(list1[:, entries]))
        for h, (cols, entries) in enumerate(halves):
            nc.scalar.activation(out=gate[:, cols], in_=b_picked[h][:], func=ACT.Tanh)
        base_sb = pool.tile([P, SLOTS], F32, name="base_sb", tag="b")
        nc.sync.dma_start(out=base_sb[:], in_=base)
        turned = pool.tile([P, SLOTS], F32, name="turned", tag="turned")
        a_picked = pool.tile([P, SLOTS], F32, name="a_picked")
        for h, (cols, entries) in enumerate(halves):
            nc.vector.tensor_tensor(out=turned[:, cols], in0=a[:].indirect(list2[:, entries]), in1=gate[:, cols], op=ALU.mult)
            nc.scalar.activation(out=a_picked[:, cols], in_=a[:].indirect(list1[:, entries]), func=ACT.Copy)

        score = pool.tile([P, SLOTS], F32, name="score")
        for h, (cols, entries) in enumerate(halves):
            nc.vector.scalar_tensor_tensor(
                out=score[:, cols], in0=turned[:, cols], scalar=lam_col[:], in1=a_picked[:, cols], op0=ALU.mult, op1=ALU.add
            )
        new_share = pool.tile([P, 1], F32, name="new_share", tag="turned")
        nc.vector.tensor_scalar(out=new_share[:], in0=trust_col[:], scalar1=256.0, scalar2=None, op0=ALU.mult)
        neg_max = pool.tile([P, 1], F32, name="neg_max")
        nc.vector.tensor_reduce(out=neg_max[:], in_=score[:], axis=AXIS.X, op=ALU.max, negate=True)

        old_sum = pool.tile([P, 1], F32, name="old_sum")
        old = pool.tile([P, SLOTS], F32, name="old", tag="gate", align_bytes=64)
        nc.scalar.activation(out=old[:], in_=earlier_sb[:], func=ACT.Copy, accum_out=old_sum[:])
        old_inv = pool.tile([P, 1], F32, name="old_inv")
        nc.vector.reciprocal(out=old_inv[:], in_=old_sum[:])
        old_share = pool.tile([P, 1], F32, name="old_share")
        nc.vector.scalar_tensor_tensor(
            out=old_share[:], in0=trust_col[:], scalar=-1.0, in1=old_inv[:], op0=ALU.add, op1=ALU.mult
        )
        carried = pool.tile([P, SLOTS], F32, name="carried")
        nc.vector.tensor_scalar(
            out=carried[:], in0=old[:], scalar1=old_share[:], scalar2=-256.0, op0=ALU.mult, op1=ALU.mult
        )

        p = pool.tile([P, SLOTS], F32, name="p")
        p_sum = pool.tile([P, 1], F32, name="p_sum")
        nc.scalar.activation(out=p[:], in_=score[:], func=ACT.Exp, bias=neg_max[:], accum_out=p_sum[:])
        p_inv = pool.tile([P, 1], F32, name="p_inv")
        nc.vector.reciprocal(out=p_inv[:], in_=p_sum[:])

        trusted = pool.tile([P, SLOTS], F32, name="trusted")
        blend = pool.tile([P, SLOTS], F32, name="blend")
        squashed = pool.tile([P, SLOTS], F32, name="squashed")
        result = pool.tile([P, SLOTS], F32, name="result")
        pieces = [slice(c, c + 128) for c in range(0, SLOTS, 128)]
        for cols in pieces:
            nc.scalar.activation(out=trusted[:, cols], in_=p[:, cols], func=ACT.Copy, scale=new_share[:])
        for cols in pieces:
            nc.vector.scalar_tensor_tensor(
                out=blend[:, cols], in0=trusted[:, cols], scalar=p_inv[:], in1=carried[:, cols], op0=ALU.mult, op1=ALU.add
            )
            nc.scalar.activation(out=squashed[:, cols], in_=blend[:, cols], func=ACT.Tanh, scale=gain_col[:])
        for n, cols in enumerate(pieces):
            nc.vector.tensor_tensor(out=result[:, cols], in0=squashed[:, cols], in1=base_sb[:, cols], op=ALU.add)
            if n > 0:
                stored = slice(0, 256) if n == 1 else cols
                nc.sync.dma_start(out=out[:, stored], in_=result[:, stored])
